import numpy as np
import ml_dtypes


def mxq(x, axis, fmt="e4m3"):
    dtype, down = {"e4m3": (ml_dtypes.float8_e4m3fn, 7), "e5m2": (ml_dtypes.float8_e5m2, 14)}[fmt]
    v = np.moveaxis(np.asarray(x, np.float32).astype(ml_dtypes.bfloat16).astype(np.float64), axis, -1)
    blocks = v.reshape(v.shape[:-1] + (-1, 32))
    amax = np.abs(blocks).max(-1, keepdims=True)
    byte = np.maximum(np.where(amax > 0, np.frexp(amax)[1] - 1 + 127, 0) - down, 1)
    scale = np.exp2(byte - 127.0)
    codes = (blocks / scale).astype(np.float32).astype(dtype).astype(np.float64)
    return np.moveaxis((codes * scale).reshape(v.shape), -1, axis)


WIDE = False


def mx_kscale(k):
    if not WIDE:
        return np.ones(k)
    levels = np.array([30, -30])
    if k % 512:
        return np.exp2(np.random.permutation(np.resize(levels, k // 32))).repeat(32)
    a = np.empty((k // 512, 16))
    for p in range(k // 512):
        a[p, :8] = np.random.permutation(np.resize(levels, 8))
        for g in range(8):
            far = levels[np.abs(levels - a[p, g]) >= 10]
            a[p, g + 8] = far[np.random.randint(len(far))]
    return np.exp2(a.ravel()).repeat(32)


def f64(x):
    return np.asarray(x).astype(np.float64)


def striped(idx):
    return np.tile(np.asarray(idx).reshape(-1, 16).T, (8, 1)).astype(np.uint16)


def unstriped(offs):
    return offs[:16].T.reshape(-1).astype(np.int64)


E2M1 = np.array([0.0, 0.5, 1.0, 1.5, 2.0, 3.0, 4.0, 6.0, -0.0, -0.5, -1.0, -1.5, -2.0, -3.0, -4.0, -6.0])


def pack_weight(w, fmt):
    k, n = w.shape
    w = f64(np.asarray(w, np.float32).astype(ml_dtypes.bfloat16)).reshape(k // 32, 32, n)
    amax = np.abs(w).max(1)
    if fmt == "e4m3":
        byte = np.frexp(amax)[1] - 1 + 127 - 7
    else:
        mant, ex = np.frexp(amax / 6.0)
        byte = np.where(mant > 0.5, ex, ex - 1) + 127
    byte = np.clip(np.where(amax > 0, byte, 1), 1, 254)
    scaled = (w * np.exp2(127.0 - byte)[:, None, :]).reshape(k, n).astype(np.float32)
    by_word = np.ascontiguousarray(scaled.reshape(k // 512, 128, 4, n).transpose(0, 1, 3, 2))
    if fmt == "e4m3":
        words = by_word.astype(ml_dtypes.float8_e4m3fn).view(np.uint8)
    else:
        c = by_word.astype(ml_dtypes.float4_e2m1fn).view(np.uint8) & 0xF
        words = (c[..., 0::2] | (c[..., 1::2] << 4)).reshape(k // 512, 128, 2 * n)
    return np.ascontiguousarray(words), np.ascontiguousarray(byte.astype(np.uint8).reshape(k // 512, 16, n))


def unpack_weight(words, scales, fmt):
    g, _, n = scales.shape
    words = np.ascontiguousarray(words).reshape(g, 128, n, -1)
    if fmt == "e4m3":
        vals = words.view(ml_dtypes.float8_e4m3fn).astype(np.float64)
    else:
        nib = np.empty((g, 128, n, 4), np.uint8)
        nib[..., 0::2] = words & 0xF
        nib[..., 1::2] = words >> 4
        vals = E2M1[nib]
    vals = vals * np.repeat(np.exp2(scales.astype(np.float64) - 127.0), 8, axis=1)[..., None]
    return vals.transpose(0, 1, 3, 2).reshape(g * 512, n)


K, T, J, I = 1024, 1024, 256, 256


def setup_inputs():
    n = np.random.standard_normal
    idx = np.random.permutation(T)[:J]
    fk = mx_kscale(K)
    kyp = pack_weight(n((K, I)) / fk[:, None], "e4m3")
    return {
        "xf": (n((K, T)) * 0.03).astype(np.float32),
        "fk": (np.random.uniform(0.5, 2.0, (K, 1)) * fk[:, None]).astype(np.float32),
        "ky_words": kyp[0],
        "ky_scales": kyp[1],
        "bi": (np.random.uniform(-0.7, 0.7, (1, I))).astype(np.float32),
        "offs": striped(idx),
    }


def reference(xf, fk, ky_words, ky_scales, bi, offs):
    idx = unstriped(offs)
    kyu = unpack_weight(ky_words, ky_scales, "e4m3")
    xg = f64(xf)[:, idx]
    x1 = np.pad(xg, ((0, 0), (1, 0)))[:, :J]
    u = (xg - 0.6 * x1) * f64(fk)
    uq = mxq(u, 0, "e5m2")
    a0 = uq.T @ kyu
    a = a0 + f64(bi)
    a1 = np.pad(a, ((0, 0), (1, 0)))[:, :I]
    y = np.abs(a - a1)
    return y

@@ -1,0 +1,132 @@
+from contextlib import ExitStack
+
+import concourse.mybir as mybir
+from concourse.masks import make_identity
+
+K, T, J, I = 1024, 1024, 256, 256
+FLOPS = 2 * K * J * I
+
+F32 = mybir.dt.float32
+BF16 = mybir.dt.bfloat16
+I32 = mybir.dt.int32
+U32 = mybir.dt.uint32
+U16 = mybir.dt.uint16
+U8 = mybir.dt.uint8
+E4M3X4 = mybir.dt.float8_e4m3fn_x4
+E5M2X4 = mybir.dt.float8_e5m2_x4
+ALU = mybir.AluOpType
+ACT = mybir.ActivationFunctionType
+
+P = 128
+PACK = 4
+PASSES = K // (P * PACK)
+HALVES = J // P
+LIST_COLS = P // 16
+LEAD = 8
+DECAY = 0.6
+
+
+def tile_list_scores_steps_given_steps_kernel(tc, xf, fk, ky_words, ky_scales, bi, offs, out):
+    nc = tc.nc
+    with ExitStack() as ctx:
+        held = ctx.enter_context(tc.tile_pool(name="held", bufs=1))
+        psum = ctx.enter_context(tc.psum_pool(name="psum", bufs=1))
+
+        planes = [(a, t) for a in range(PASSES) for t in range(PACK)]
+        x_rows = xf.rearrange("(a p t) n -> a t p n", a=PASSES, t=PACK)
+        x_sb = {at: held.tile([P, T], F32, name="x%d%d" % at) for at in planes}
+        offsets = held.tile([P, J // 16], U16, name="offsets")
+        fk_sb = held.tile([P, PASSES, PACK], F32, name="fk_sb")
+        bi_sb = held.tile([P, 2], F32, name="bi_sb")
+        key_words = held.tile([P, PASSES, I], I32, name="key_words", align_bytes=64)
+        key_scales = held.tile([P, PASSES, I], U8, name="key_scales", align_bytes=64)
+
+        for n, (a, t) in enumerate(planes):
+            nc.sync.dma_start(out=x_sb[(a, t)][:], in_=x_rows[a, t])
+            if n == 0:
+                nc.sync.dma_start(offsets[:], offs)
+        nc.sync.dma_start(out=key_words[:], in_=ky_words.rearrange("a p n r -> p a (n r)").bitcast(I32))
+        nc.scalar.dma_start(out=fk_sb[:], in_=fk.rearrange("(a p t) o -> p a (t o)", a=PASSES, t=PACK))
+
+        nc.gpsimd.dma_start(out=bi_sb[:], in_=bi.rearrange("o (p c) -> p (o c)", c=2))
+        nc.gpsimd.memset(key_scales[:].bitcast(I32), 0)
+        for q in range(4):
+            nc.gpsimd.dma_start(
+                out=key_scales[32 * q : 32 * q + 4].bitcast(I32),
+                in_=ky_scales[:, 4 * q : 4 * q + 4, :].rearrange("a r n -> r a n").bitcast(I32),
+            )
+
+        ident = held.tile([P, P], F32, name="ident")
+        make_identity(nc, ident[:])
+        bias_ps = psum.tile([P, 2, P], F32, name="bias_ps")
+        for c in range(2):
+            nc.tensor.transpose(bias_ps[:, c, :], bi_sb[:, c : c + 1].to_broadcast([P, P]), ident[:])
+        bias = held.tile([P, I], F32, name="bias")
+        nc.vector.tensor_copy(
+            out=bias[:].rearrange("p (n c) -> p n c", c=2), in_=bias_ps[:].rearrange("p c n -> p n c")
+        )
+
+        picked = {at: held.tile([P, LEAD + J], F32, name="picked%d%d" % at) for at in planes}
+        for at in planes:
+            nc.vector.memset(picked[at][:, LEAD - 1 : LEAD], 0.0)
+        scores = [held.tile([P, LEAD + I], F32, name="scores%d" % h) for h in range(HALVES)]
+        for h in range(HALVES):
+            nc.vector.memset(scores[h][:, LEAD - 1 : LEAD], 0.0)
+
+        acc = [psum.tile([P, I], F32, name="acc%d" % h) for h in range(HALVES)]
+        for a in range(PASSES):
+            woven = [
+                held.tile([P, P * PACK], BF16, name="woven%d%d" % (a, h), align_bytes=64) for h in range(HALVES)
+            ]
+            for t in range(PACK):
+                g = picked[(a, t)]
+                diffs = []
+                for h in range(HALVES):
+                    nc.scalar.activation(
+                        g[:, LEAD + P * h : LEAD + P * (h + 1)],
+                        x_sb[(a, t)][:].indirect(offsets[:, LIST_COLS * h : LIST_COLS * (h + 1)]),
+                        ACT.Copy,
+                    )
+                for h in range(HALVES):
+                    d = held.tile([P, P], F32, name="diff%d%d%d" % (a, t, h))
+                    nc.vector.scalar_tensor_tensor(
+                        out=d[:],
+                        in0=g[:, LEAD - 1 + P * h : LEAD - 1 + P * (h + 1)],
+                        scalar=-DECAY,
+                        in1=g[:, LEAD + P * h : LEAD + P * (h + 1)],
+                        op0=ALU.mult,
+                        op1=ALU.add,
+                    )
+                    diffs.append(d)
+                for h in range(HALVES):
+                    nc.vector.tensor_scalar(
+                        out=woven[h][:, t :: PACK],
+                        in0=diffs[h][:],
+                        scalar1=fk_sb[:, a, t : t + 1],
+                        scalar2=None,
+                        op0=ALU.mult,
+                    )
+            for h in range(HALVES):
+                u_words = held.tile([P, P], U32, name="u_words%d%d" % (a, h), align_bytes=64)
+                u_scales = held.tile([P, P], U8, name="u_scales%d%d" % (a, h), align_bytes=64)
+                nc.vector.quantize_mx(out=u_words[:].bitcast(E5M2X4), scales=u_scales[:], in_=woven[h][:])
+                nc.tensor.matmul_mx(
+                    out=acc[h][:],
+                    lhsT=u_words[:].bitcast(E5M2X4),
+                    lhsT_scale=u_scales[:],
+                    rhs=key_words[:, a, :].bitcast(E4M3X4),
+                    rhs_scale=key_scales[:, a, :],
+                    start=(a == 0),
+                    stop=(a == PASSES - 1),
+                )
+
+        steps = [held.tile([P, I], F32, name="steps%d" % h) for h in range(HALVES)]
+        for h in range(HALVES):
+            nc.vector.tensor_tensor(out=scores[h][:, LEAD:], in0=acc[h][:], in1=bias[:], op=ALU.add)
+        for h in range(HALVES):
+            nc.vector.tensor_tensor(
+                out=steps[h][:], in0=scores[h][:, LEAD:], in1=scores[h][:, LEAD - 1 : LEAD - 1 + I], op=ALU.subtract
+            )
+            result = held.tile([P, I], F32, name="result%d" % h)
+            nc.scalar.activation(result[:], steps[h][:], ACT.Abs)
+            nc.sync.dma_start(out=out[P * h : P * (h + 1), :], in_=result[:])

@@ -21,9 +21,11 @@ P = 128
 PACK = 4
 PASSES = K // (P * PACK)
 HALVES = J // P
-LIST_COLS = P // 16
 LEAD = 8
 DECAY = 0.6
+LOADS = [[0,1],[2,3],[4],[5],[6],[7]]
+COLS = 128
+TAIL_PIECES = 4
 
 
 def tile_list_scores_steps_given_steps_kernel(tc, xf, fk, ky_words, ky_scales, bi, offs, out):
@@ -32,32 +34,44 @@ def tile_list_scores_steps_given_steps_kernel(tc, xf, fk, ky_words, ky_scales, b
         held = ctx.enter_context(tc.tile_pool(name="held", bufs=1))
         psum = ctx.enter_context(tc.psum_pool(name="psum", bufs=1))
 
-        planes = [(a, t) for a in range(PASSES) for t in range(PACK)]
-        x_rows = xf.rearrange("(a p t) n -> a t p n", a=PASSES, t=PACK)
-        x_sb = {at: held.tile([P, T], F32, name="x%d%d" % at) for at in planes}
+        x_rows = xf.rearrange("(a p t) n -> a p t n", a=PASSES, t=PACK)
         offsets = held.tile([P, J // 16], U16, name="offsets")
         fk_sb = held.tile([P, PASSES, PACK], F32, name="fk_sb")
         bi_sb = held.tile([P, 2], F32, name="bi_sb")
         key_words = held.tile([P, PASSES, I], I32, name="key_words", align_bytes=64)
         key_scales = held.tile([P, PASSES, I], U8, name="key_scales", align_bytes=64)
 
-        for n, (a, t) in enumerate(planes):
-            nc.sync.dma_start(out=x_sb[(a, t)][:], in_=x_rows[a, t])
+        window = {}
+        for n, group in enumerate(LOADS):
+            a, t0 = divmod(group[0], PACK)
+            x_sb = held.tile([P, len(group) * T], F32, name="x%d" % n)
+            nc.sync.dma_start(
+                out=x_sb[:], in_=x_rows[a, :, t0 : t0 + len(group), :].rearrange("p t n -> p (t n)")
+            )
+            for s in range(len(group)):
+                window[(a, t0 + s)] = x_sb[:, s * T : (s + 1) * T]
             if n == 0:
                 nc.sync.dma_start(offsets[:], offs)
         nc.sync.dma_start(out=key_words[:], in_=ky_words.rearrange("a p n r -> p a (n r)").bitcast(I32))
         nc.scalar.dma_start(out=fk_sb[:], in_=fk.rearrange("(a p t) o -> p a (t o)", a=PASSES, t=PACK))
+        nc.scalar.dma_start(out=bi_sb[:], in_=bi.rearrange("o (p c) -> p (o c)", c=2))
 
-        nc.gpsimd.dma_start(out=bi_sb[:], in_=bi.rearrange("o (p c) -> p (o c)", c=2))
-        nc.gpsimd.memset(key_scales[:].bitcast(I32), 0)
+        zero = held.tile([P, 1], F32, name="zero")
+        nc.vector.memset(zero[:], 0.0)
+        picked = {at: held.tile([P, LEAD + J], F32, name="picked%d%d" % at) for at in window}
+        scores = [held.tile([P, LEAD + I], F32, name="scores%d" % h) for h in range(HALVES)]
+        for tile in list(picked.values()) + scores:
+            nc.scalar.activation(tile[:, LEAD - 1 : LEAD], zero[:], ACT.Copy)
+
+        ident = held.tile([P, P], F32, name="ident")
+        make_identity(nc, ident[:])
+        nc.vector.memset(key_scales[:].bitcast(I32), 0)
         for q in range(4):
             nc.gpsimd.dma_start(
                 out=key_scales[32 * q : 32 * q + 4].bitcast(I32),
                 in_=ky_scales[:, 4 * q : 4 * q + 4, :].rearrange("a r n -> r a n").bitcast(I32),
             )
 
-        ident = held.tile([P, P], F32, name="ident")
-        make_identity(nc, ident[:])
         bias_ps = psum.tile([P, 2, P], F32, name="bias_ps")
         for c in range(2):
             nc.tensor.transpose(bias_ps[:, c, :], bi_sb[:, c : c + 1].to_broadcast([P, P]), ident[:])
@@ -66,42 +80,38 @@ def tile_list_scores_steps_given_steps_kernel(tc, xf, fk, ky_words, ky_scales, b
             out=bias[:].rearrange("p (n c) -> p n c", c=2), in_=bias_ps[:].rearrange("p c n -> p n c")
         )
 
-        picked = {at: held.tile([P, LEAD + J], F32, name="picked%d%d" % at) for at in planes}
-        for at in planes:
-            nc.vector.memset(picked[at][:, LEAD - 1 : LEAD], 0.0)
-        scores = [held.tile([P, LEAD + I], F32, name="scores%d" % h) for h in range(HALVES)]
-        for h in range(HALVES):
-            nc.vector.memset(scores[h][:, LEAD - 1 : LEAD], 0.0)
-
-        acc = [psum.tile([P, I], F32, name="acc%d" % h) for h in range(HALVES)]
+        parts = [(h, c0) for h in range(HALVES) for c0 in range(0, I, COLS)]
+        acc = {hc: psum.tile([P, COLS], F32, name="acc%d_%d" % hc) for hc in parts}
         for a in range(PASSES):
             woven = [
                 held.tile([P, P * PACK], BF16, name="woven%d%d" % (a, h), align_bytes=64) for h in range(HALVES)
             ]
             for t in range(PACK):
                 g = picked[(a, t)]
-                diffs = []
-                for h in range(HALVES):
-                    nc.scalar.activation(
-                        g[:, LEAD + P * h : LEAD + P * (h + 1)],
-                        x_sb[(a, t)][:].indirect(offsets[:, LIST_COLS * h : LIST_COLS * (h + 1)]),
-                        ACT.Copy,
-                    )
-                for h in range(HALVES):
-                    d = held.tile([P, P], F32, name="diff%d%d%d" % (a, t, h))
+                last = (a, t) == (PASSES - 1, PACK - 1)
+                width = J // (TAIL_PIECES if last else HALVES)
+                diffs = {}
+                for j0 in range(0, J, width):
+                    source = window[(a, t)].indirect(offsets[:, j0 // 16 : (j0 + width) // 16])
+                    if False:
+                        nc.vector.tensor_copy(g[:, LEAD + j0 : LEAD + j0 + width], source)
+                    else:
+                        nc.scalar.activation(g[:, LEAD + j0 : LEAD + j0 + width], source, ACT.Copy)
+                for j0 in range(0, J, width):
+                    diffs[j0] = held.tile([P, width], F32, name="diff%d%d_%d" % (a, t, j0))
                     nc.vector.scalar_tensor_tensor(
-                        out=d[:],
-                        in0=g[:, LEAD - 1 + P * h : LEAD - 1 + P * (h + 1)],
+                        out=diffs[j0][:],
+                        in0=g[:, LEAD - 1 + j0 : LEAD - 1 + j0 + width],
                         scalar=-DECAY,
-                        in1=g[:, LEAD + P * h : LEAD + P * (h + 1)],
+                        in1=g[:, LEAD + j0 : LEAD + j0 + width],
                         op0=ALU.mult,
                         op1=ALU.add,
                     )
-                    diffs.append(d)
-                for h in range(HALVES):
+                for j0 in range(0, J, width):
+                    h, jh = divmod(j0, P)
                     nc.vector.tensor_scalar(
-                        out=woven[h][:, t :: PACK],
-                        in0=diffs[h][:],
+                        out=woven[h][:, PACK * jh + t : PACK * (jh + width) : PACK],
+                        in0=diffs[j0][:],
                         scalar1=fk_sb[:, a, t : t + 1],
                         scalar2=None,
                         op0=ALU.mult,
@@ -110,23 +120,32 @@ def tile_list_scores_steps_given_steps_kernel(tc, xf, fk, ky_words, ky_scales, b
                 u_words = held.tile([P, P], U32, name="u_words%d%d" % (a, h), align_bytes=64)
                 u_scales = held.tile([P, P], U8, name="u_scales%d%d" % (a, h), align_bytes=64)
                 nc.vector.quantize_mx(out=u_words[:].bitcast(E5M2X4), scales=u_scales[:], in_=woven[h][:])
-                nc.tensor.matmul_mx(
-                    out=acc[h][:],
-                    lhsT=u_words[:].bitcast(E5M2X4),
-                    lhsT_scale=u_scales[:],
-                    rhs=key_words[:, a, :].bitcast(E4M3X4),
-                    rhs_scale=key_scales[:, a, :],
-                    start=(a == 0),
-                    stop=(a == PASSES - 1),
-                )
+                for c0 in range(0, I, COLS):
+                    nc.tensor.matmul_mx(
+                        out=acc[(h, c0)][:],
+                        lhsT=u_words[:].bitcast(E5M2X4),
+                        lhsT_scale=u_scales[:],
+                        rhs=key_words[:, a, c0 : c0 + COLS].bitcast(E4M3X4),
+                        rhs_scale=key_scales[:, a, c0 : c0 + COLS],
+                        start=(a == 0),
+                        stop=(a == PASSES - 1),
+                    )
 
-        steps = [held.tile([P, I], F32, name="steps%d" % h) for h in range(HALVES)]
-        for h in range(HALVES):
-            nc.vector.tensor_tensor(out=scores[h][:, LEAD:], in0=acc[h][:], in1=bias[:], op=ALU.add)
-        for h in range(HALVES):
+        for h, c0 in parts:
             nc.vector.tensor_tensor(
-                out=steps[h][:], in0=scores[h][:, LEAD:], in1=scores[h][:, LEAD - 1 : LEAD - 1 + I], op=ALU.subtract
+                out=scores[h][:, LEAD + c0 : LEAD + c0 + COLS],
+                in0=acc[(h, c0)][:],
+                in1=bias[:, c0 : c0 + COLS],
+                op=ALU.add,
             )
-            result = held.tile([P, I], F32, name="result%d" % h)
-            nc.scalar.activation(result[:], steps[h][:], ACT.Abs)
-            nc.sync.dma_start(out=out[P * h : P * (h + 1), :], in_=result[:])
+        for h, c0 in parts:
+            steps = held.tile([P, COLS], F32, name="steps%d_%d" % (h, c0))
+            nc.vector.tensor_tensor(
+                out=steps[:],
+                in0=scores[h][:, LEAD + c0 : LEAD + c0 + COLS],
+                in1=scores[h][:, LEAD - 1 + c0 : LEAD - 1 + c0 + COLS],
+                op=ALU.subtract,
+            )
+            result = held.tile([P, COLS], F32, name="result%d_%d" % (h, c0))
+            nc.scalar.activation(result[:], steps[:], ACT.Abs)
+            nc.sync.dma_start(out=out[P * h : P * (h + 1), c0 : c0 + COLS], in_=result[:])

@@ -23,7 +23,7 @@ PASSES = K // (P * PACK)
 HALVES = J // P
 LEAD = 8
 DECAY = 0.6
-LOADS = [[0,1],[2,3],[4],[5],[6],[7]]
+LOADS = [[0],[1],[2],[3],[4],[5],[6],[7]]
 COLS = 128
 TAIL_PIECES = 4
 
@@ -52,6 +52,12 @@ def tile_list_scores_steps_given_steps_kernel(tc, xf, fk, ky_words, ky_scales, b
                 window[(a, t0 + s)] = x_sb[:, s * T : (s + 1) * T]
             if n == 0:
                 nc.sync.dma_start(offsets[:], offs)
+        nc.vector.memset(key_scales[:].bitcast(I32), 0)
+        for q in range(4):
+            nc.sync.dma_start(
+                out=key_scales[32 * q : 32 * q + 4].bitcast(I32),
+                in_=ky_scales[:, 4 * q : 4 * q + 4, :].rearrange("a r n -> r a n").bitcast(I32),
+            )
         nc.sync.dma_start(out=key_words[:], in_=ky_words.rearrange("a p n r -> p a (n r)").bitcast(I32))
         nc.scalar.dma_start(out=fk_sb[:], in_=fk.rearrange("(a p t) o -> p a (t o)", a=PASSES, t=PACK))
         nc.scalar.dma_start(out=bi_sb[:], in_=bi.rearrange("o (p c) -> p (o c)", c=2))
@@ -65,12 +71,6 @@ def tile_list_scores_steps_given_steps_kernel(tc, xf, fk, ky_words, ky_scales, b
 
         ident = held.tile([P, P], F32, name="ident")
         make_identity(nc, ident[:])
-        nc.vector.memset(key_scales[:].bitcast(I32), 0)
-        for q in range(4):
-            nc.gpsimd.dma_start(
-                out=key_scales[32 * q : 32 * q + 4].bitcast(I32),
-                in_=ky_scales[:, 4 * q : 4 * q + 4, :].rearrange("a r n -> r a n").bitcast(I32),
-            )
 
         bias_ps = psum.tile([P, 2, P], F32, name="bias_ps")
         for c in range(2):

from contextlib import ExitStack

import concourse.mybir as mybir
from concourse.masks import make_identity

K, T, J, I = 1024, 1024, 256, 256
FLOPS = 2 * K * J * I

F32 = mybir.dt.float32
BF16 = mybir.dt.bfloat16
I32 = mybir.dt.int32
U32 = mybir.dt.uint32
U16 = mybir.dt.uint16
U8 = mybir.dt.uint8
E4M3X4 = mybir.dt.float8_e4m3fn_x4
E5M2X4 = mybir.dt.float8_e5m2_x4
ALU = mybir.AluOpType
ACT = mybir.ActivationFunctionType

P = 128
PACK = 4
PASSES = K // (P * PACK)
HALVES = J // P
LEAD = 8
DECAY = 0.6
LOADS = [[0],[1],[2],[3],[4],[5],[6],[7]]
COLS = 128
TAIL_PIECES = 4


def tile_list_scores_steps_given_steps_kernel(tc, xf, fk, ky_words, ky_scales, bi, offs, out):
    nc = tc.nc
    with ExitStack() as ctx:
        held = ctx.enter_context(tc.tile_pool(name="held", bufs=1))
        psum = ctx.enter_context(tc.psum_pool(name="psum", bufs=1))

        x_rows = xf.rearrange("(a p t) n -> a p t n", a=PASSES, t=PACK)
        offsets = held.tile([P, J // 16], U16, name="offsets")
        fk_sb = held.tile([P, PASSES, PACK], F32, name="fk_sb")
        bi_sb = held.tile([P, 2], F32, name="bi_sb")
        key_words = held.tile([P, PASSES, I], I32, name="key_words", align_bytes=64)
        key_scales = held.tile([P, PASSES, I], U8, name="key_scales", align_bytes=64)

        window = {}
        for n, group in enumerate(LOADS):
            a, t0 = divmod(group[0], PACK)
            x_sb = held.tile([P, len(group) * T], F32, name="x%d" % n)
            nc.sync.dma_start(
                out=x_sb[:], in_=x_rows[a, :, t0 : t0 + len(group), :].rearrange("p t n -> p (t n)")
            )
            for s in range(len(group)):
                window[(a, t0 + s)] = x_sb[:, s * T : (s + 1) * T]
            if n == 0:
                nc.sync.dma_start(offsets[:], offs)
        nc.vector.memset(key_scales[:].bitcast(I32), 0)
        for q in range(4):
            nc.sync.dma_start(
                out=key_scales[32 * q : 32 * q + 4].bitcast(I32),
                in_=ky_scales[:, 4 * q : 4 * q + 4, :].rearrange("a r n -> r a n").bitcast(I32),
            )
        nc.sync.dma_start(out=key_words[:], in_=ky_words.rearrange("a p n r -> p a (n r)").bitcast(I32))
        nc.scalar.dma_start(out=fk_sb[:], in_=fk.rearrange("(a p t) o -> p a (t o)", a=PASSES, t=PACK))
        nc.scalar.dma_start(out=bi_sb[:], in_=bi.rearrange("o (p c) -> p (o c)", c=2))

        zero = held.tile([P, 1], F32, name="zero")
        nc.vector.memset(zero[:], 0.0)
        picked = {at: held.tile([P, LEAD + J], F32, name="picked%d%d" % at) for at in window}
        scores = [held.tile([P, LEAD + I], F32, name="scores%d" % h) for h in range(HALVES)]
        for tile in list(picked.values()) + scores:
            nc.scalar.activation(tile[:, LEAD - 1 : LEAD], zero[:], ACT.Copy)

        ident = held.tile([P, P], F32, name="ident")
        make_identity(nc, ident[:])

        bias_ps = psum.tile([P, 2, P], F32, name="bias_ps")
        for c in range(2):
            nc.tensor.transpose(bias_ps[:, c, :], bi_sb[:, c : c + 1].to_broadcast([P, P]), ident[:])
        bias = held.tile([P, I], F32, name="bias")
        nc.vector.tensor_copy(
            out=bias[:].rearrange("p (n c) -> p n c", c=2), in_=bias_ps[:].rearrange("p c n -> p n c")
        )

        parts = [(h, c0) for h in range(HALVES) for c0 in range(0, I, COLS)]
        acc = {hc: psum.tile([P, COLS], F32, name="acc%d_%d" % hc) for hc in parts}
        for a in range(PASSES):
            woven = [
                held.tile([P, P * PACK], BF16, name="woven%d%d" % (a, h), align_bytes=64) for h in range(HALVES)
            ]
            for t in range(PACK):
                g = picked[(a, t)]
                last = (a, t) == (PASSES - 1, PACK - 1)
                width = J // (TAIL_PIECES if last else HALVES)
                diffs = {}
                for j0 in range(0, J, width):
                    source = window[(a, t)].indirect(offsets[:, j0 // 16 : (j0 + width) // 16])
                    if False:
                        nc.vector.tensor_copy(g[:, LEAD + j0 : LEAD + j0 + width], source)
                    else:
                        nc.scalar.activation(g[:, LEAD + j0 : LEAD + j0 + width], source, ACT.Copy)
                for j0 in range(0, J, width):
                    diffs[j0] = held.tile([P, width], F32, name="diff%d%d_%d" % (a, t, j0))
                    nc.vector.scalar_tensor_tensor(
                        out=diffs[j0][:],
                        in0=g[:, LEAD - 1 + j0 : LEAD - 1 + j0 + width],
                        scalar=-DECAY,
                        in1=g[:, LEAD + j0 : LEAD + j0 + width],
                        op0=ALU.mult,
                        op1=ALU.add,
                    )
                for j0 in range(0, J, width):
                    h, jh = divmod(j0, P)
                    nc.vector.tensor_scalar(
                        out=woven[h][:, PACK * jh + t : PACK * (jh + width) : PACK],
                        in0=diffs[j0][:],
                        scalar1=fk_sb[:, a, t : t + 1],
                        scalar2=None,
                        op0=ALU.mult,
                    )
            for h in range(HALVES):
                u_words = held.tile([P, P], U32, name="u_words%d%d" % (a, h), align_bytes=64)
                u_scales = held.tile([P, P], U8, name="u_scales%d%d" % (a, h), align_bytes=64)
                nc.vector.quantize_mx(out=u_words[:].bitcast(E5M2X4), scales=u_scales[:], in_=woven[h][:])
                for c0 in range(0, I, COLS):
                    nc.tensor.matmul_mx(
                        out=acc[(h, c0)][:],
                        lhsT=u_words[:].bitcast(E5M2X4),
                        lhsT_scale=u_scales[:],
                        rhs=key_words[:, a, c0 : c0 + COLS].bitcast(E4M3X4),
                        rhs_scale=key_scales[:, a, c0 : c0 + COLS],
                        start=(a == 0),
                        stop=(a == PASSES - 1),
                    )

        for h, c0 in parts:
            nc.vector.tensor_tensor(
                out=scores[h][:, LEAD + c0 : LEAD + c0 + COLS],
                in0=acc[(h, c0)][:],
                in1=bias[:, c0 : c0 + COLS],
                op=ALU.add,
            )
        for h, c0 in parts:
            steps = held.tile([P, COLS], F32, name="steps%d_%d" % (h, c0))
            nc.vector.tensor_tensor(
                out=steps[:],
                in0=scores[h][:, LEAD + c0 : LEAD + c0 + COLS],
                in1=scores[h][:, LEAD - 1 + c0 : LEAD - 1 + c0 + COLS],
                op=ALU.subtract,
            )
            result = held.tile([P, COLS], F32, name="result%d_%d" % (h, c0))
            nc.scalar.activation(result[:], steps[:], ACT.Abs)
            nc.sync.dma_start(out=out[P * h : P * (h + 1), c0 : c0 + COLS], in_=result[:])
